import numpy as np
import ml_dtypes


def mxq(x, axis, fmt="e4m3"):
    dtype, down = {"e4m3": (ml_dtypes.float8_e4m3fn, 7), "e5m2": (ml_dtypes.float8_e5m2, 14)}[fmt]
    v = np.moveaxis(np.asarray(x, np.float32).astype(ml_dtypes.bfloat16).astype(np.float64), axis, -1)
    blocks = v.reshape(v.shape[:-1] + (-1, 32))
    amax = np.abs(blocks).max(-1, keepdims=True)
    byte = np.maximum(np.where(amax > 0, np.frexp(amax)[1] - 1 + 127, 0) - down, 1)
    scale = np.exp2(byte - 127.0)
    codes = (blocks / scale).astype(np.float32).astype(dtype).astype(np.float64)
    return np.moveaxis((codes * scale).reshape(v.shape), -1, axis)


WIDE = False


def mx_kscale(k):
    if not WIDE:
        return np.ones(k)
    levels = np.array([10, -10, 5, -5, 0])
    if k % 512:
        return np.exp2(np.random.permutation(np.resize(levels, k // 32))).repeat(32)
    a = np.empty((k // 512, 16))
    for p in range(k // 512):
        a[p, :8] = np.random.permutation(np.resize(levels, 8))
        for g in range(8):
            far = levels[np.abs(levels - a[p, g]) >= 10]
            a[p, g + 8] = far[np.random.randint(len(far))]
    return np.exp2(a.ravel()).repeat(32)


def f64(x):
    return np.asarray(x).astype(np.float64)


def striped(idx):
    return np.tile(idx.reshape(-1, 16).T, (8, 1)).astype(np.uint16)


def unstriped(offs):
    return offs[:16].T.reshape(-1).astype(np.int64)


def striped8(idx):
    return np.concatenate([x.reshape(-1, 16).T for x in idx]).astype(np.uint16)


def runs(offs, k):
    lists = np.stack([offs[16 * r : 16 * r + 16].T.reshape(-1) for r in range(8)]).astype(np.int64)
    return lists[np.arange(k) % 512 // 64]


def pack_weight(w):
    k, n = w.shape
    w = f64(np.asarray(w, np.float32).astype(ml_dtypes.bfloat16)).reshape(k // 32, 32, n)
    amax = np.abs(w).max(1)
    byte = np.clip(np.where(amax > 0, np.frexp(amax)[1] - 1 + 127 - 7, 1), 1, 254)
    scaled = (w * np.exp2(127.0 - byte)[:, None, :]).reshape(k, n).astype(np.float32)
    words = np.ascontiguousarray(scaled.reshape(k // 512, 128, 4, n).transpose(0, 1, 3, 2)).astype(ml_dtypes.float8_e4m3fn).view(np.uint8)
    return words, np.ascontiguousarray(byte.astype(np.uint8).reshape(k // 512, 16, n))


def unpack_weight(words, scales):
    g, p, n, _ = words.shape
    vals = np.ascontiguousarray(words).view(ml_dtypes.float8_e4m3fn).astype(np.float64) * np.repeat(np.exp2(scales.astype(np.float64) - 127.0), 8, axis=1)[..., None]
    return vals.transpose(0, 1, 3, 2).reshape(g * 512, n)

def planes(y):
    n, m = y.shape
    v = y.astype(np.float32).astype(ml_dtypes.bfloat16).astype(np.float64).reshape(n // 32, 32, m)
    top = np.abs(v).max(1)
    byte = np.clip(np.where(top > 0, np.frexp(top)[1] - 1 + 127 - 7, 1), 1, 254)
    codes = (v * np.exp2(127.0 - byte)[:, None, :]).reshape(n, m).astype(np.float32).astype(ml_dtypes.float8_e4m3fn).view(np.uint8)
    words = codes.reshape(n // 512, 128, 4, m).transpose(0, 1, 3, 2)
    return np.ascontiguousarray(words), np.ascontiguousarray(byte.astype(np.uint8).reshape(n // 512, 16, m))


K, T, S, H, W, C = 512, 2048, 256, 512, 128, 512


def setup_inputs():
    n = np.random.standard_normal
    s = mx_kscale(K)[:, None]
    packed_xT = pack_weight(n((K, T)) * s)
    packed_w1 = pack_weight(n((K, H)) / np.sqrt(K) / s)
    perm = np.random.permutation(S)
    return {
        "x_words": packed_xT[0],
        "x_scales": packed_xT[1],
        "w1_words": packed_w1[0],
        "w1_scales": packed_w1[1],
        "gs": (np.random.uniform(0.5, 1.5, (K, 1)) / s).astype(np.float32),
        "offs": striped(np.random.permutation(T)[:S]),
        "n1": striped(perm[:W]),
        "n2": striped(perm[W:]),
        "ca": striped(np.random.permutation(T)[:C]),
        "hc": striped8(np.random.randint(0, T, (8, C))),
        "n3": striped8(np.stack([np.random.permutation(S) for _ in range(8)])),
        "n4": striped8(np.stack([np.random.permutation(S) for _ in range(8)])),
    }


def reference(x_words, x_scales, w1_words, w1_scales, gs, offs, n1, n2, ca, hc, n3, n4):
    x_ca = unpack_weight(x_words, x_scales)[:, unstriped(ca)]
    xq = unpack_weight(x_words, x_scales)[:, unstriped(offs)]
    y = unpack_weight(w1_words, w1_scales).T @ xq
    pb = y[:, unstriped(n2)]
    pa = y[:, unstriped(n1)]
    rb = pb - (0.5 * pa)
    ra = np.sqrt((pa) ** 2 + (pb) ** 2 + 0.25)
    ds = np.zeros((H, S))
    ds[:, unstriped(n1)] = ra
    dt = ds.copy()
    dt[:, unstriped(n2)] = rb
    z = f64(gs) * dt
    zq = mxq(z, 0, "e4m3")
    a = 0.0625 * (x_ca.T @ zq)
    x_hc = unpack_weight(x_words, x_scales)[np.arange(K)[:, None], runs(hc, K)]
    b = 0.0625 * (x_hc.T @ zq)
    out_0 = a[np.arange(C)[:, None], runs(n3, C)] - (np.tanh(b) * (b[np.arange(C)[:, None], runs(n4, C)]))
    return (out_0,) + planes(out_0)

@@ -1,0 +1,200 @@
+from contextlib import ExitStack
+
+import concourse.mybir as mybir
+
+F32 = mybir.dt.float32
+BF16 = mybir.dt.bfloat16
+I32 = mybir.dt.int32
+U32 = mybir.dt.uint32
+U16 = mybir.dt.uint16
+U8 = mybir.dt.uint8
+FP8X4 = mybir.dt.float8_e4m3fn_x4
+ALU = mybir.AluOpType
+ACT = mybir.ActivationFunctionType
+
+P = 128
+PACK = 4
+QUADS = 4
+T, S, H, W, C = 2048, 256, 512, 128, 512
+FLOPS = 2 * 512 * (H * S + 2 * C * S)
+
+
+def tile_picked_cdhsoftbpolar_none_po_kernel(
+    tc, x_words, x_scales, w1_words, w1_scales, gs, offs, n1, n2, ca, hc, n3, n4, out_0, out_1, out_2
+):
+    nc = tc.nc
+    with ExitStack() as ctx:
+        lists = ctx.enter_context(tc.tile_pool(name="lists", bufs=1))
+        sb = ctx.enter_context(tc.tile_pool(name="sb", bufs=1))
+        psum = ctx.enter_context(tc.psum_pool(name="psum", bufs=1))
+
+        def tile(name, shape, dtype, tag=None):
+            return sb.tile(shape, dtype, name=name, tag=tag or name, align_bytes=64)
+
+        def load_list(name, src):
+            dst = lists.tile(list(src.shape), U16, name=name)
+            nc.sync.dma_start(dst[:], src)
+            return dst
+
+        def deal(dst, src):
+            nc.vector.tensor_copy(
+                out=dst.rearrange("p (t m) -> p t m", t=PACK), in_=src.rearrange("p (m t) -> p t m", t=PACK)
+            )
+
+        x_rows = x_scales[0].bitcast(I32)
+        w_rows = w1_scales[0].bitcast(I32)
+
+        ws = tile("ws", [P, H], U8)
+        nc.gpsimd.memset(ws[:].bitcast(I32), 0)
+        xs = tile("xs", [P, T], U8)
+        nc.vector.memset(xs[:].bitcast(I32), 0)
+        offs_sb = load_list("offs_sb", offs)
+        for q in range(QUADS):
+            nc.sync.dma_start(ws[32 * q : 32 * q + 4, :].bitcast(I32), w_rows[4 * q : 4 * q + 4, :])
+        xw = tile("xw", [P, T], U32)
+        nc.sync.dma_start(xw[:].bitcast(I32), x_words[0].rearrange("p n t -> p (n t)").bitcast(I32))
+        for q in range(QUADS):
+            nc.sync.dma_start(xs[32 * q : 32 * q + 4, :].bitcast(I32), x_rows[4 * q : 4 * q + 4, :])
+        ww = tile("ww", [P, H], I32)
+        nc.sync.dma_start(ww[:], w1_words[0].rearrange("p n t -> p (n t)").bitcast(I32))
+        n1_sb = load_list("n1_sb", n1)
+        n2_sb = load_list("n2_sb", n2)
+        ca_sb = load_list("ca_sb", ca)
+        hc_sb = load_list("hc_sb", hc)
+        xs8 = tile("xs8", [P, T], U8)
+        nc.vector.memset(xs8[:].bitcast(I32), 0)
+        nc.sync.dma_start(xs8[0:P:8, :].bitcast(I32), x_rows)
+        gs_sb = tile("gs_sb", [P, PACK], F32)
+        nc.sync.dma_start(gs_sb[:], gs.rearrange("(p t) o -> p (t o)", t=PACK))
+        n3_sb = load_list("n3_sb", n3)
+        n4_sb = load_list("n4_sb", n4)
+
+        hs = tile("hs", [P, C], U8)
+        nc.vector.memset(hs[:].bitcast(I32), 0)
+        a_sb = [tile(f"a_sb{t}", [P, 2 * S], F32) for t in range(PACK)]
+        b_sb = [tile(f"b_sb{t}", [P, 2 * S], F32) for t in range(PACK)]
+        for t in range(PACK):
+            nc.vector.memset(a_sb[t][:, S:], 0.0)
+            nc.vector.memset(b_sb[t][:, S:], 0.0)
+
+        q_s = tile("q_s", [P, S], U8)
+        nc.vector.tensor_copy(q_s[:], xs[:].indirect(offs_sb[:]))
+        q_w = tile("q_w", [P, S], U32)
+        nc.vector.tensor_copy(q_w[:], xw[:].indirect(offs_sb[:]))
+        ws_d = tile("ws_d", [P, H], U8)
+        deal(ws_d[:], ws[:])
+        y_sb = []
+        for t in range(PACK):
+            ww_t = tile(f"ww_d{t}", [P, P], I32)
+            nc.vector.tensor_copy(ww_t[:], ww[:, t:H:PACK])
+            y_ps = psum.tile([P, S], F32, name=f"y_ps{t}", tag=f"bank{t}")
+            nc.tensor.matmul_mx(
+                out=y_ps[:],
+                lhsT=ww_t[:].bitcast(FP8X4),
+                lhsT_scale=ws_d[:, t * P : (t + 1) * P],
+                rhs=q_w[:].bitcast(FP8X4),
+                rhs_scale=q_s[:],
+                start=True,
+                stop=True,
+            )
+            y_t = tile(f"y_sb{t}", [P, S], F32)
+            nc.vector.tensor_copy(y_t[:], y_ps[:])
+            y_sb.append(y_t)
+
+        dts = []
+        for t in range(PACK):
+            pab = tile(f"pab{t}", [P, 2 * W], F32)
+            nc.scalar.activation(pab[:, :W], y_sb[t][:].indirect(n1_sb[:]), ACT.Copy)
+            nc.scalar.activation(pab[:, W:], y_sb[t][:].indirect(n2_sb[:]), ACT.Copy)
+            sq = tile(f"sq{t}", [P, 2 * W], F32)
+            nc.vector.tensor_tensor(sq[:], pab[:], pab[:], ALU.mult)
+            rb = tile(f"rb{t}", [P, W], F32)
+            nc.vector.scalar_tensor_tensor(rb[:], pab[:, :W], -0.5, pab[:, W:], ALU.mult, ALU.add)
+            ss = tile(f"ss{t}", [P, W], F32)
+            nc.vector.scalar_tensor_tensor(ss[:], sq[:, :W], 0.25, sq[:, W:], ALU.add, ALU.add)
+            ra = tile(f"ra{t}", [P, W], F32)
+            nc.scalar.activation(ra[:], ss[:], ACT.Sqrt)
+            dt_t = tile(f"dt{t}", [P, S], F32)
+            nc.scalar.activation(dt_t[:].indirect(n2_sb[:]), rb[:], ACT.Copy)
+            nc.scalar.activation(dt_t[:].indirect(n1_sb[:]), ra[:], ACT.Copy)
+            dts.append(dt_t)
+
+        c_sg = tile("c_sg", [P, C], U8, tag="sq0")
+        nc.vector.tensor_copy(c_sg[:], xs[:].indirect(ca_sb[:]))
+        h_sg = tile("h_sg", [P, C], U8, tag="sq1")
+        nc.vector.tensor_copy(h_sg[:], xs8[:].indirect(hc_sb[:]))
+        h_sd = tile("h_sd", [P, C], U8)
+        deal(h_sd[:], h_sg[:])
+        for r in range(4):
+            nc.sync.dma_start(hs[r:P:32, :].bitcast(I32), h_sd[8 * r : P : 32, :].bitcast(I32))
+        cs = tile("cs", [P, C], U8)
+        deal(cs[:], c_sg[:])
+        h_wg = tile("h_wg", [P, C], U32, tag="sq2")
+        nc.vector.tensor_copy(h_wg[:], xw[:].indirect(hc_sb[:]))
+        c_wg = tile("c_wg", [P, C], U32, tag="sq3")
+        nc.vector.tensor_copy(c_wg[:], xw[:].indirect(ca_sb[:]))
+        hw = tile("hw", [P, C], I32)
+        deal(hw[:], h_wg[:].bitcast(I32))
+        cw = tile("cw", [P, C], I32, tag="sq2")
+        deal(cw[:], c_wg[:].bitcast(I32))
+
+        zb = tile("zb", [P, S, PACK], BF16, tag="sq3")
+        for t in range(PACK):
+            nc.vector.tensor_scalar(zb[:, :, t], dts[t][:], gs_sb[:, t : t + 1], None, ALU.mult)
+        z_w = tile("z_w", [P, S], U32)
+        z_s = tile("z_s", [P, S], U8)
+        nc.vector.quantize_mx(out=z_w[:].bitcast(FP8X4), scales=z_s[:], in_=zb[:].rearrange("p j t -> p (j t)"))
+
+        o_sb = tile("o_sb", [P, PACK, S], F32)
+        ob = tile("ob", [P, S, PACK], BF16)
+        o_w = tile("o_w", [P, S], U32)
+        o_s = tile("o_s", [P, S], U8)
+        out_rows = out_0.rearrange("(p t) j -> p t j", t=PACK)
+        out_words = out_1[0].rearrange("p n t -> p (n t)").bitcast(I32)
+        out_scales = out_2[0].bitcast(I32)
+        th, ga, gb, prod = [], [], [], []
+        for t in range(PACK):
+            cols = slice(t * P, (t + 1) * P)
+            b_ps = psum.tile([P, S], F32, name=f"b_ps{t}", tag=f"bank{4 + t}")
+            nc.tensor.matmul_mx(
+                out=b_ps[:], lhsT=hw[:, cols].bitcast(FP8X4), lhsT_scale=hs[:, cols],
+                rhs=z_w[:].bitcast(FP8X4), rhs_scale=z_s[:], start=True, stop=True,
+            )
+            a_ps = psum.tile([P, S], F32, name=f"a_ps{t}", tag=f"bank{t}")
+            nc.tensor.matmul_mx(
+                out=a_ps[:], lhsT=cw[:, cols].bitcast(FP8X4), lhsT_scale=cs[:, cols],
+                rhs=z_w[:].bitcast(FP8X4), rhs_scale=z_s[:], start=True, stop=True,
+            )
+            nc.vector.tensor_scalar(b_sb[t][:, :S], b_ps[:], 0.0625, None, ALU.mult)
+            nc.vector.tensor_scalar(a_sb[t][:, :S], a_ps[:], 0.0625, None, ALU.mult)
+            th.append(tile(f"th{t}", [P, S], F32))
+            nc.scalar.activation(th[t][:], b_sb[t][:, :S], ACT.Tanh)
+            ga.append(tile(f"ga{t}", [P, S], F32))
+            gb.append(tile(f"gb{t}", [P, S], F32))
+            prod.append(tile(f"prod{t}", [P, S], F32))
+
+        def combine(t, js):
+            entries = slice(js.start // 16, js.stop // 16)
+            nc.scalar.activation(gb[t][:, js], b_sb[t][:].indirect(n4_sb[:, entries]), ACT.Copy)
+            nc.scalar.activation(ga[t][:, js], a_sb[t][:].indirect(n3_sb[:, entries]), ACT.Copy)
+            nc.vector.tensor_tensor(prod[t][:, js], th[t][:, js], gb[t][:, js], ALU.mult)
+            nc.vector.tensor_tensor(o_sb[:, t, js], ga[t][:, js], prod[t][:, js], ALU.subtract)
+
+        for t in range(2):
+            combine(t, slice(0, S))
+        nc.sync.dma_start(out_rows[:, 0:2, :], o_sb[:, 0:2, :])
+        for j0 in range(0, S, S // 2):
+            js = slice(j0, j0 + S // 2)
+            for t in range(2, PACK):
+                combine(t, js)
+            nc.sync.dma_start(out_rows[:, 2:PACK, js], o_sb[:, 2:PACK, js])
+            nc.vector.tensor_copy(ob[:, js, :], o_sb[:, :, js].rearrange("p t j -> p j t"))
+            nc.vector.quantize_mx(
+                out=o_w[:, js].bitcast(FP8X4),
+                scales=o_s[:, js],
+                in_=ob[:, js, :].rearrange("p j t -> p (j t)"),
+            )
+            nc.sync.dma_start(out_words[:, js], o_w[:, js].bitcast(I32))
+        for q in range(QUADS):
+            queue = nc.scalar if q < 2 else nc.sync
+            queue.dma_start(out_scales[4 * q : 4 * q + 4, :], o_s[32 * q : 32 * q + 4, :].bitcast(I32))

@@ -44,54 +44,55 @@ def tile_picked_cdhsoftbpolar_none_po_kernel(
         x_rows = x_scales[0].bitcast(I32)
         w_rows = w1_scales[0].bitcast(I32)
 
-        ws = tile("ws", [P, H], U8)
-        nc.gpsimd.memset(ws[:].bitcast(I32), 0)
         xs = tile("xs", [P, T], U8)
         nc.vector.memset(xs[:].bitcast(I32), 0)
         offs_sb = load_list("offs_sb", offs)
-        for q in range(QUADS):
-            nc.sync.dma_start(ws[32 * q : 32 * q + 4, :].bitcast(I32), w_rows[4 * q : 4 * q + 4, :])
         xw = tile("xw", [P, T], U32)
         nc.sync.dma_start(xw[:].bitcast(I32), x_words[0].rearrange("p n t -> p (n t)").bitcast(I32))
-        for q in range(QUADS):
-            nc.sync.dma_start(xs[32 * q : 32 * q + 4, :].bitcast(I32), x_rows[4 * q : 4 * q + 4, :])
         ww = tile("ww", [P, H], I32)
         nc.sync.dma_start(ww[:], w1_words[0].rearrange("p n t -> p (n t)").bitcast(I32))
+        ws = tile("ws", [P, H], U8)
+        for q in range(QUADS):
+            rows = w_rows[4 * q : 4 * q + 4, :].unsqueeze(0).broadcast_to([8, 4, H // 4])
+            queue = nc.sync if q < 2 else nc.gpsimd
+            queue.dma_start(ws[32 * q : 32 * q + 32, :].bitcast(I32), rows)
+        for q in range(QUADS):
+            nc.sync.dma_start(xs[32 * q : 32 * q + 4, :].bitcast(I32), x_rows[4 * q : 4 * q + 4, :])
         n1_sb = load_list("n1_sb", n1)
         n2_sb = load_list("n2_sb", n2)
         ca_sb = load_list("ca_sb", ca)
         hc_sb = load_list("hc_sb", hc)
         xs8 = tile("xs8", [P, T], U8)
-        nc.vector.memset(xs8[:].bitcast(I32), 0)
+        nc.gpsimd.memset(xs8[:].bitcast(I32), 0)
         nc.sync.dma_start(xs8[0:P:8, :].bitcast(I32), x_rows)
         gs_sb = tile("gs_sb", [P, PACK], F32)
         nc.sync.dma_start(gs_sb[:], gs.rearrange("(p t) o -> p (t o)", t=PACK))
         n3_sb = load_list("n3_sb", n3)
         n4_sb = load_list("n4_sb", n4)
 
-        hs = tile("hs", [P, C], U8)
-        nc.vector.memset(hs[:].bitcast(I32), 0)
-        a_sb = [tile(f"a_sb{t}", [P, 2 * S], F32) for t in range(PACK)]
-        b_sb = [tile(f"b_sb{t}", [P, 2 * S], F32) for t in range(PACK)]
-        for t in range(PACK):
-            nc.vector.memset(a_sb[t][:, S:], 0.0)
-            nc.vector.memset(b_sb[t][:, S:], 0.0)
+        a_sb = [tile(f"a_sb{t}", [P, S], F32) for t in range(PACK)]
+        b_sb = [tile(f"b_sb{t}", [P, S], F32) for t in range(PACK)]
+        one = tile("one", [P, 1], F32)
+        nc.vector.memset(one[:], 1.0)
+
+        warm_sqrt = tile("warm_sqrt", [P, 1], F32)
+        nc.scalar.activation(warm_sqrt[:], one[:], ACT.Sqrt)
 
         q_s = tile("q_s", [P, S], U8)
         nc.vector.tensor_copy(q_s[:], xs[:].indirect(offs_sb[:]))
         q_w = tile("q_w", [P, S], U32)
         nc.vector.tensor_copy(q_w[:], xw[:].indirect(offs_sb[:]))
-        ws_d = tile("ws_d", [P, H], U8)
-        deal(ws_d[:], ws[:])
         y_sb = []
         for t in range(PACK):
-            ww_t = tile(f"ww_d{t}", [P, P], I32)
+            ww_t = tile(f"ww_d{t}", [P, P], I32, tag=f"ww_d{t % 2}")
             nc.vector.tensor_copy(ww_t[:], ww[:, t:H:PACK])
+            ws_t = tile(f"ws_d{t}", [P, P], U8)
+            nc.vector.tensor_copy(ws_t[:], ws[:, t:H:PACK])
             y_ps = psum.tile([P, S], F32, name=f"y_ps{t}", tag=f"bank{t}")
             nc.tensor.matmul_mx(
                 out=y_ps[:],
                 lhsT=ww_t[:].bitcast(FP8X4),
-                lhsT_scale=ws_d[:, t * P : (t + 1) * P],
+                lhsT_scale=ws_t[:],
                 rhs=q_w[:].bitcast(FP8X4),
                 rhs_scale=q_s[:],
                 start=True,
@@ -107,43 +108,50 @@ def tile_picked_cdhsoftbpolar_none_po_kernel(
             nc.scalar.activation(pab[:, :W], y_sb[t][:].indirect(n1_sb[:]), ACT.Copy)
             nc.scalar.activation(pab[:, W:], y_sb[t][:].indirect(n2_sb[:]), ACT.Copy)
             sq = tile(f"sq{t}", [P, 2 * W], F32)
-            nc.vector.tensor_tensor(sq[:], pab[:], pab[:], ALU.mult)
+            nc.gpsimd.tensor_tensor(sq[:], pab[:], pab[:], ALU.mult)
             rb = tile(f"rb{t}", [P, W], F32)
             nc.vector.scalar_tensor_tensor(rb[:], pab[:, :W], -0.5, pab[:, W:], ALU.mult, ALU.add)
             ss = tile(f"ss{t}", [P, W], F32)
-            nc.vector.scalar_tensor_tensor(ss[:], sq[:, :W], 0.25, sq[:, W:], ALU.add, ALU.add)
+            nc.gpsimd.tensor_tensor(ss[:], sq[:, :W], sq[:, W:], ALU.add)
             ra = tile(f"ra{t}", [P, W], F32)
-            nc.scalar.activation(ra[:], ss[:], ACT.Sqrt)
+            nc.scalar.activation(ra[:], ss[:], ACT.Sqrt, bias=0.25)
             dt_t = tile(f"dt{t}", [P, S], F32)
             nc.scalar.activation(dt_t[:].indirect(n2_sb[:]), rb[:], ACT.Copy)
             nc.scalar.activation(dt_t[:].indirect(n1_sb[:]), ra[:], ACT.Copy)
             dts.append(dt_t)
 
-        c_sg = tile("c_sg", [P, C], U8, tag="sq0")
+        c_sg = tile("c_sg", [P, C], U8, tag="ws_d3")
         nc.vector.tensor_copy(c_sg[:], xs[:].indirect(ca_sb[:]))
-        h_sg = tile("h_sg", [P, C], U8, tag="sq1")
+        h_sg = tile("h_sg", [P, C], U8, tag="pab0")
         nc.vector.tensor_copy(h_sg[:], xs8[:].indirect(hc_sb[:]))
-        h_sd = tile("h_sd", [P, C], U8)
-        deal(h_sd[:], h_sg[:])
+        both = tile("both", [P, C], U8)
+        nc.vector.tensor_copy(both[:].bitcast(I32), c_sg[:].bitcast(I32))
         for r in range(4):
-            nc.sync.dma_start(hs[r:P:32, :].bitcast(I32), h_sd[8 * r : P : 32, :].bitcast(I32))
-        cs = tile("cs", [P, C], U8)
-        deal(cs[:], c_sg[:])
-        h_wg = tile("h_wg", [P, C], U32, tag="sq2")
+            nc.sync.dma_start(both[4 + r : P : 32, :].bitcast(I32), h_sg[8 * r : P : 32, :].bitcast(I32))
+        h_wg = tile("h_wg", [P, C], U32, tag="pab1")
         nc.vector.tensor_copy(h_wg[:], xw[:].indirect(hc_sb[:]))
-        c_wg = tile("c_wg", [P, C], U32, tag="sq3")
+        c_wg = tile("c_wg", [P, C], U32, tag="pab2")
         nc.vector.tensor_copy(c_wg[:], xw[:].indirect(ca_sb[:]))
         hw = tile("hw", [P, C], I32)
         deal(hw[:], h_wg[:].bitcast(I32))
-        cw = tile("cw", [P, C], I32, tag="sq2")
+        cw = tile("cw", [P, C], I32, tag="pab1")
         deal(cw[:], c_wg[:].bitcast(I32))
 
-        zb = tile("zb", [P, S, PACK], BF16, tag="sq3")
+        planes = tile("planes", [P, C], U8, tag="pab2")
+        deal(planes[:], both[:])
+        zb = tile("zb", [P, S, PACK], BF16, tag="both")
+        halves = [slice(0, S // 2), slice(S // 2, S)]
         for t in range(PACK):
-            nc.vector.tensor_scalar(zb[:, :, t], dts[t][:], gs_sb[:, t : t + 1], None, ALU.mult)
+            for js in halves if t == PACK - 1 else [slice(0, S)]:
+                nc.vector.tensor_scalar(zb[:, js, t], dts[t][:, js], gs_sb[:, t : t + 1], None, ALU.mult)
+        warm_tanh = tile("warm_tanh", [P, 1], F32)
+        nc.scalar.activation(warm_tanh[:], dts[PACK - 1][:, 0:1], ACT.Tanh)
         z_w = tile("z_w", [P, S], U32)
         z_s = tile("z_s", [P, S], U8)
-        nc.vector.quantize_mx(out=z_w[:].bitcast(FP8X4), scales=z_s[:], in_=zb[:].rearrange("p j t -> p (j t)"))
+        for js in halves:
+            nc.vector.quantize_mx(
+                out=z_w[:, js].bitcast(FP8X4), scales=z_s[:, js], in_=zb[:, js, :].rearrange("p j t -> p (j t)")
+            )
 
         o_sb = tile("o_sb", [P, PACK, S], F32)
         ob = tile("ob", [P, S, PACK], BF16)
@@ -156,28 +164,35 @@ def tile_picked_cdhsoftbpolar_none_po_kernel(
         for t in range(PACK):
             cols = slice(t * P, (t + 1) * P)
             b_ps = psum.tile([P, S], F32, name=f"b_ps{t}", tag=f"bank{4 + t}")
-            nc.tensor.matmul_mx(
-                out=b_ps[:], lhsT=hw[:, cols].bitcast(FP8X4), lhsT_scale=hs[:, cols],
-                rhs=z_w[:].bitcast(FP8X4), rhs_scale=z_s[:], start=True, stop=True,
-            )
             a_ps = psum.tile([P, S], F32, name=f"a_ps{t}", tag=f"bank{t}")
-            nc.tensor.matmul_mx(
-                out=a_ps[:], lhsT=cw[:, cols].bitcast(FP8X4), lhsT_scale=cs[:, cols],
-                rhs=z_w[:].bitcast(FP8X4), rhs_scale=z_s[:], start=True, stop=True,
-            )
-            nc.vector.tensor_scalar(b_sb[t][:, :S], b_ps[:], 0.0625, None, ALU.mult)
-            nc.vector.tensor_scalar(a_sb[t][:, :S], a_ps[:], 0.0625, None, ALU.mult)
+            products = [(b_ps, hw, 4), (a_ps, cw, 0)]
+            for acc, words, first_row in products[::-1] if t == 0 else products:
+                nc.tensor.matmul_mx(
+                    out=acc[:], lhsT=words[:, cols].bitcast(FP8X4), lhsT_scale=planes[first_row:P, cols],
+                    rhs=z_w[:].bitcast(FP8X4), rhs_scale=z_s[:], start=True, stop=True,
+                )
             th.append(tile(f"th{t}", [P, S], F32))
-            nc.scalar.activation(th[t][:], b_sb[t][:, :S], ACT.Tanh)
+            if t == 0:
+                nc.scalar.activation(th[t][:], b_ps[:], ACT.Tanh, scale=0.0625)
+                nc.vector.tensor_scalar(a_sb[t][:, :S], a_ps[:], 0.0625, None, ALU.mult)
+                nc.vector.tensor_scalar(b_sb[t][:, :S], b_ps[:], 0.0625, None, ALU.mult)
+            else:
+                nc.vector.tensor_scalar(b_sb[t][:, :S], b_ps[:], 0.0625, None, ALU.mult)
+                nc.vector.tensor_scalar(a_sb[t][:, :S], a_ps[:], 0.0625, None, ALU.mult)
+                nc.scalar.activation(th[t][:], b_sb[t][:, :S], ACT.Tanh)
             ga.append(tile(f"ga{t}", [P, S], F32))
             gb.append(tile(f"gb{t}", [P, S], F32))
             prod.append(tile(f"prod{t}", [P, S], F32))
 
-        def combine(t, js):
-            entries = slice(js.start // 16, js.stop // 16)
-            nc.scalar.activation(gb[t][:, js], b_sb[t][:].indirect(n4_sb[:, entries]), ACT.Copy)
-            nc.scalar.activation(ga[t][:, js], a_sb[t][:].indirect(n3_sb[:, entries]), ACT.Copy)
+        def combine(t, js, rounded=None):
+            fetches = [(gb[t], b_sb[t], n4_sb), (ga[t], a_sb[t], n3_sb)]
+            for dst, window, places in fetches[::-1] if t == 0 else fetches:
+                for j0 in range(js.start, js.stop, W):
+                    entries = places[:, j0 // 16 : (j0 + W) // 16]
+                    nc.scalar.activation(dst[:, j0 : j0 + W], window[:].indirect(entries), ACT.Copy)
             nc.vector.tensor_tensor(prod[t][:, js], th[t][:, js], gb[t][:, js], ALU.mult)
+            if rounded is not None:
+                nc.vector.tensor_tensor(rounded, ga[t][:, js], prod[t][:, js], ALU.subtract)
             nc.vector.tensor_tensor(o_sb[:, t, js], ga[t][:, js], prod[t][:, js], ALU.subtract)
 
         for t in range(2):
@@ -185,10 +200,14 @@ def tile_picked_cdhsoftbpolar_none_po_kernel(
         nc.sync.dma_start(out_rows[:, 0:2, :], o_sb[:, 0:2, :])
         for j0 in range(0, S, S // 2):
             js = slice(j0, j0 + S // 2)
-            for t in range(2, PACK):
-                combine(t, js)
+            combine(2, js)
+            if j0 == 0:
+                combine(3, js)
+                nc.vector.tensor_copy(ob[:, js, :], o_sb[:, :, js].rearrange("p t j -> p j t"))
+            else:
+                nc.vector.tensor_copy(ob[:, js, 0:3], o_sb[:, 0:3, js].rearrange("p t j -> p j t"))
+                combine(3, js, ob[:, js, 3])
             nc.sync.dma_start(out_rows[:, 2:PACK, js], o_sb[:, 2:PACK, js])
-            nc.vector.tensor_copy(ob[:, js, :], o_sb[:, :, js].rearrange("p t j -> p j t"))
             nc.vector.quantize_mx(
                 out=o_w[:, js].bitcast(FP8X4),
                 scales=o_s[:, js],

@@ -70,8 +70,8 @@ def tile_picked_cdhsoftbpolar_none_po_kernel(
         n3_sb = load_list("n3_sb", n3)
         n4_sb = load_list("n4_sb", n4)
 
-        a_sb = [tile(f"a_sb{t}", [P, S], F32) for t in range(PACK)]
-        b_sb = [tile(f"b_sb{t}", [P, S], F32) for t in range(PACK)]
+        a_sb = [tile(f"a_sb{t}", [P, 2 * S], F32) for t in range(PACK)]
+        b_sb = [tile(f"b_sb{t}", [P, 2 * S], F32) for t in range(PACK)]
         one = tile("one", [P, 1], F32)
         nc.vector.memset(one[:], 1.0)
 
@@ -107,17 +107,17 @@ def tile_picked_cdhsoftbpolar_none_po_kernel(
             pab = tile(f"pab{t}", [P, 2 * W], F32)
             nc.scalar.activation(pab[:, :W], y_sb[t][:].indirect(n1_sb[:]), ACT.Copy)
             nc.scalar.activation(pab[:, W:], y_sb[t][:].indirect(n2_sb[:]), ACT.Copy)
-            sq = tile(f"sq{t}", [P, 2 * W], F32)
-            nc.gpsimd.tensor_tensor(sq[:], pab[:], pab[:], ALU.mult)
-            rb = tile(f"rb{t}", [P, W], F32)
-            nc.vector.scalar_tensor_tensor(rb[:], pab[:, :W], -0.5, pab[:, W:], ALU.mult, ALU.add)
+            sq = b_sb[t][:, S:]
+            nc.gpsimd.tensor_tensor(sq, pab[:], pab[:], ALU.mult)
+            rb = a_sb[t][:, S : S + W]
+            nc.vector.scalar_tensor_tensor(rb, pab[:, :W], -0.5, pab[:, W:], ALU.mult, ALU.add)
             ss = tile(f"ss{t}", [P, W], F32)
             nc.gpsimd.tensor_tensor(ss[:], sq[:, :W], sq[:, W:], ALU.add)
-            ra = tile(f"ra{t}", [P, W], F32)
-            nc.scalar.activation(ra[:], ss[:], ACT.Sqrt, bias=0.25)
+            ra = a_sb[t][:, S + W :]
+            nc.scalar.activation(ra, ss[:], ACT.Sqrt, bias=0.25)
             dt_t = tile(f"dt{t}", [P, S], F32)
-            nc.scalar.activation(dt_t[:].indirect(n2_sb[:]), rb[:], ACT.Copy)
-            nc.scalar.activation(dt_t[:].indirect(n1_sb[:]), ra[:], ACT.Copy)
+            nc.scalar.activation(dt_t[:].indirect(n2_sb[:]), rb, ACT.Copy)
+            nc.scalar.activation(dt_t[:].indirect(n1_sb[:]), ra, ACT.Copy)
             dts.append(dt_t)
 
         c_sg = tile("c_sg", [P, C], U8, tag="ws_d3")
@@ -184,36 +184,24 @@ def tile_picked_cdhsoftbpolar_none_po_kernel(
             gb.append(tile(f"gb{t}", [P, S], F32))
             prod.append(tile(f"prod{t}", [P, S], F32))
 
-        def combine(t, js, rounded=None):
+        last = PACK - 1
+        for t in range(PACK):
             fetches = [(gb[t], b_sb[t], n4_sb), (ga[t], a_sb[t], n3_sb)]
             for dst, window, places in fetches[::-1] if t == 0 else fetches:
-                for j0 in range(js.start, js.stop, W):
-                    entries = places[:, j0 // 16 : (j0 + W) // 16]
-                    nc.scalar.activation(dst[:, j0 : j0 + W], window[:].indirect(entries), ACT.Copy)
-            nc.vector.tensor_tensor(prod[t][:, js], th[t][:, js], gb[t][:, js], ALU.mult)
-            if rounded is not None:
-                nc.vector.tensor_tensor(rounded, ga[t][:, js], prod[t][:, js], ALU.subtract)
-            nc.vector.tensor_tensor(o_sb[:, t, js], ga[t][:, js], prod[t][:, js], ALU.subtract)
-
-        for t in range(2):
-            combine(t, slice(0, S))
-        nc.sync.dma_start(out_rows[:, 0:2, :], o_sb[:, 0:2, :])
-        for j0 in range(0, S, S // 2):
-            js = slice(j0, j0 + S // 2)
-            combine(2, js)
-            if j0 == 0:
-                combine(3, js)
-                nc.vector.tensor_copy(ob[:, js, :], o_sb[:, :, js].rearrange("p t j -> p j t"))
-            else:
-                nc.vector.tensor_copy(ob[:, js, 0:3], o_sb[:, 0:3, js].rearrange("p t j -> p j t"))
-                combine(3, js, ob[:, js, 3])
-            nc.sync.dma_start(out_rows[:, 2:PACK, js], o_sb[:, 2:PACK, js])
+                nc.scalar.activation(dst[:], window[:].indirect(places[:]), ACT.Copy)
+            nc.vector.tensor_tensor(prod[t][:], th[t][:], gb[t][:], ALU.mult)
+            for js in halves if t == last else [slice(0, S)]:
+                nc.vector.tensor_tensor(o_sb[:, t, js], ga[t][:, js], prod[t][:, js], ALU.subtract)
+            nc.sync.dma_start(out_rows[:, t, :], o_sb[:, t, :])
+            if t == last - 1:
+                nc.vector.tensor_copy(ob[:, :, :last], o_sb[:, :last, :].rearrange("p t j -> p j t"))
+        for js in halves:
+            nc.vector.tensor_copy(ob[:, js, last], o_sb[:, last, js])
+        for js in halves:
             nc.vector.quantize_mx(
-                out=o_w[:, js].bitcast(FP8X4),
-                scales=o_s[:, js],
-                in_=ob[:, js, :].rearrange("p j t -> p (j t)"),
+                out=o_w[:, js].bitcast(FP8X4), scales=o_s[:, js], in_=ob[:, js, :].rearrange("p j t -> p (j t)")
             )
-            nc.sync.dma_start(out_words[:, js], o_w[:, js].bitcast(I32))
+        nc.scalar.dma_start(out_words, o_w[:].bitcast(I32))
         for q in range(QUADS):
-            queue = nc.scalar if q < 2 else nc.sync
+            queue = nc.scalar if q < 1 else nc.sync
             queue.dma_start(out_scales[4 * q : 4 * q + 4, :], o_s[32 * q : 32 * q + 4, :].bitcast(I32))

from contextlib import ExitStack

import concourse.mybir as mybir

F32 = mybir.dt.float32
BF16 = mybir.dt.bfloat16
I32 = mybir.dt.int32
U32 = mybir.dt.uint32
U16 = mybir.dt.uint16
U8 = mybir.dt.uint8
FP8X4 = mybir.dt.float8_e4m3fn_x4
ALU = mybir.AluOpType
ACT = mybir.ActivationFunctionType

P = 128
PACK = 4
QUADS = 4
T, S, H, W, C = 2048, 256, 512, 128, 512
FLOPS = 2 * 512 * (H * S + 2 * C * S)


def tile_picked_cdhsoftbpolar_none_po_kernel(
    tc, x_words, x_scales, w1_words, w1_scales, gs, offs, n1, n2, ca, hc, n3, n4, out_0, out_1, out_2
):
    nc = tc.nc
    with ExitStack() as ctx:
        lists = ctx.enter_context(tc.tile_pool(name="lists", bufs=1))
        sb = ctx.enter_context(tc.tile_pool(name="sb", bufs=1))
        psum = ctx.enter_context(tc.psum_pool(name="psum", bufs=1))

        def tile(name, shape, dtype, tag=None):
            return sb.tile(shape, dtype, name=name, tag=tag or name, align_bytes=64)

        def load_list(name, src):
            dst = lists.tile(list(src.shape), U16, name=name)
            nc.sync.dma_start(dst[:], src)
            return dst

        def deal(dst, src):
            nc.vector.tensor_copy(
                out=dst.rearrange("p (t m) -> p t m", t=PACK), in_=src.rearrange("p (m t) -> p t m", t=PACK)
            )

        x_rows = x_scales[0].bitcast(I32)
        w_rows = w1_scales[0].bitcast(I32)

        xs = tile("xs", [P, T], U8)
        nc.vector.memset(xs[:].bitcast(I32), 0)
        offs_sb = load_list("offs_sb", offs)
        xw = tile("xw", [P, T], U32)
        nc.sync.dma_start(xw[:].bitcast(I32), x_words[0].rearrange("p n t -> p (n t)").bitcast(I32))
        ww = tile("ww", [P, H], I32)
        nc.sync.dma_start(ww[:], w1_words[0].rearrange("p n t -> p (n t)").bitcast(I32))
        ws = tile("ws", [P, H], U8)
        for q in range(QUADS):
            rows = w_rows[4 * q : 4 * q + 4, :].unsqueeze(0).broadcast_to([8, 4, H // 4])
            queue = nc.sync if q < 2 else nc.gpsimd
            queue.dma_start(ws[32 * q : 32 * q + 32, :].bitcast(I32), rows)
        for q in range(QUADS):
            nc.sync.dma_start(xs[32 * q : 32 * q + 4, :].bitcast(I32), x_rows[4 * q : 4 * q + 4, :])
        n1_sb = load_list("n1_sb", n1)
        n2_sb = load_list("n2_sb", n2)
        ca_sb = load_list("ca_sb", ca)
        hc_sb = load_list("hc_sb", hc)
        xs8 = tile("xs8", [P, T], U8)
        nc.gpsimd.memset(xs8[:].bitcast(I32), 0)
        nc.sync.dma_start(xs8[0:P:8, :].bitcast(I32), x_rows)
        gs_sb = tile("gs_sb", [P, PACK], F32)
        nc.sync.dma_start(gs_sb[:], gs.rearrange("(p t) o -> p (t o)", t=PACK))
        n3_sb = load_list("n3_sb", n3)
        n4_sb = load_list("n4_sb", n4)

        a_sb = [tile(f"a_sb{t}", [P, 2 * S], F32) for t in range(PACK)]
        b_sb = [tile(f"b_sb{t}", [P, 2 * S], F32) for t in range(PACK)]
        one = tile("one", [P, 1], F32)
        nc.vector.memset(one[:], 1.0)

        warm_sqrt = tile("warm_sqrt", [P, 1], F32)
        nc.scalar.activation(warm_sqrt[:], one[:], ACT.Sqrt)

        q_s = tile("q_s", [P, S], U8)
        nc.vector.tensor_copy(q_s[:], xs[:].indirect(offs_sb[:]))
        q_w = tile("q_w", [P, S], U32)
        nc.vector.tensor_copy(q_w[:], xw[:].indirect(offs_sb[:]))
        y_sb = []
        for t in range(PACK):
            ww_t = tile(f"ww_d{t}", [P, P], I32, tag=f"ww_d{t % 2}")
            nc.vector.tensor_copy(ww_t[:], ww[:, t:H:PACK])
            ws_t = tile(f"ws_d{t}", [P, P], U8)
            nc.vector.tensor_copy(ws_t[:], ws[:, t:H:PACK])
            y_ps = psum.tile([P, S], F32, name=f"y_ps{t}", tag=f"bank{t}")
            nc.tensor.matmul_mx(
                out=y_ps[:],
                lhsT=ww_t[:].bitcast(FP8X4),
                lhsT_scale=ws_t[:],
                rhs=q_w[:].bitcast(FP8X4),
                rhs_scale=q_s[:],
                start=True,
                stop=True,
            )
            y_t = tile(f"y_sb{t}", [P, S], F32)
            nc.vector.tensor_copy(y_t[:], y_ps[:])
            y_sb.append(y_t)

        dts = []
        for t in range(PACK):
            pab = tile(f"pab{t}", [P, 2 * W], F32)
            nc.scalar.activation(pab[:, :W], y_sb[t][:].indirect(n1_sb[:]), ACT.Copy)
            nc.scalar.activation(pab[:, W:], y_sb[t][:].indirect(n2_sb[:]), ACT.Copy)
            sq = b_sb[t][:, S:]
            nc.gpsimd.tensor_tensor(sq, pab[:], pab[:], ALU.mult)
            rb = a_sb[t][:, S : S + W]
            nc.vector.scalar_tensor_tensor(rb, pab[:, :W], -0.5, pab[:, W:], ALU.mult, ALU.add)
            ss = tile(f"ss{t}", [P, W], F32)
            nc.gpsimd.tensor_tensor(ss[:], sq[:, :W], sq[:, W:], ALU.add)
            ra = a_sb[t][:, S + W :]
            nc.scalar.activation(ra, ss[:], ACT.Sqrt, bias=0.25)
            dt_t = tile(f"dt{t}", [P, S], F32)
            nc.scalar.activation(dt_t[:].indirect(n2_sb[:]), rb, ACT.Copy)
            nc.scalar.activation(dt_t[:].indirect(n1_sb[:]), ra, ACT.Copy)
            dts.append(dt_t)

        c_sg = tile("c_sg", [P, C], U8, tag="ws_d3")
        nc.vector.tensor_copy(c_sg[:], xs[:].indirect(ca_sb[:]))
        h_sg = tile("h_sg", [P, C], U8, tag="pab0")
        nc.vector.tensor_copy(h_sg[:], xs8[:].indirect(hc_sb[:]))
        both = tile("both", [P, C], U8)
        nc.vector.tensor_copy(both[:].bitcast(I32), c_sg[:].bitcast(I32))
        for r in range(4):
            nc.sync.dma_start(both[4 + r : P : 32, :].bitcast(I32), h_sg[8 * r : P : 32, :].bitcast(I32))
        h_wg = tile("h_wg", [P, C], U32, tag="pab1")
        nc.vector.tensor_copy(h_wg[:], xw[:].indirect(hc_sb[:]))
        c_wg = tile("c_wg", [P, C], U32, tag="pab2")
        nc.vector.tensor_copy(c_wg[:], xw[:].indirect(ca_sb[:]))
        hw = tile("hw", [P, C], I32)
        deal(hw[:], h_wg[:].bitcast(I32))
        cw = tile("cw", [P, C], I32, tag="pab1")
        deal(cw[:], c_wg[:].bitcast(I32))

        planes = tile("planes", [P, C], U8, tag="pab2")
        deal(planes[:], both[:])
        zb = tile("zb", [P, S, PACK], BF16, tag="both")
        halves = [slice(0, S // 2), slice(S // 2, S)]
        for t in range(PACK):
            for js in halves if t == PACK - 1 else [slice(0, S)]:
                nc.vector.tensor_scalar(zb[:, js, t], dts[t][:, js], gs_sb[:, t : t + 1], None, ALU.mult)
        warm_tanh = tile("warm_tanh", [P, 1], F32)
        nc.scalar.activation(warm_tanh[:], dts[PACK - 1][:, 0:1], ACT.Tanh)
        z_w = tile("z_w", [P, S], U32)
        z_s = tile("z_s", [P, S], U8)
        for js in halves:
            nc.vector.quantize_mx(
                out=z_w[:, js].bitcast(FP8X4), scales=z_s[:, js], in_=zb[:, js, :].rearrange("p j t -> p (j t)")
            )

        o_sb = tile("o_sb", [P, PACK, S], F32)
        ob = tile("ob", [P, S, PACK], BF16)
        o_w = tile("o_w", [P, S], U32)
        o_s = tile("o_s", [P, S], U8)
        out_rows = out_0.rearrange("(p t) j -> p t j", t=PACK)
        out_words = out_1[0].rearrange("p n t -> p (n t)").bitcast(I32)
        out_scales = out_2[0].bitcast(I32)
        th, ga, gb, prod = [], [], [], []
        for t in range(PACK):
            cols = slice(t * P, (t + 1) * P)
            b_ps = psum.tile([P, S], F32, name=f"b_ps{t}", tag=f"bank{4 + t}")
            a_ps = psum.tile([P, S], F32, name=f"a_ps{t}", tag=f"bank{t}")
            products = [(b_ps, hw, 4), (a_ps, cw, 0)]
            for acc, words, first_row in products[::-1] if t == 0 else products:
                nc.tensor.matmul_mx(
                    out=acc[:], lhsT=words[:, cols].bitcast(FP8X4), lhsT_scale=planes[first_row:P, cols],
                    rhs=z_w[:].bitcast(FP8X4), rhs_scale=z_s[:], start=True, stop=True,
                )
            th.append(tile(f"th{t}", [P, S], F32))
            if t == 0:
                nc.scalar.activation(th[t][:], b_ps[:], ACT.Tanh, scale=0.0625)
                nc.vector.tensor_scalar(a_sb[t][:, :S], a_ps[:], 0.0625, None, ALU.mult)
                nc.vector.tensor_scalar(b_sb[t][:, :S], b_ps[:], 0.0625, None, ALU.mult)
            else:
                nc.vector.tensor_scalar(b_sb[t][:, :S], b_ps[:], 0.0625, None, ALU.mult)
                nc.vector.tensor_scalar(a_sb[t][:, :S], a_ps[:], 0.0625, None, ALU.mult)
                nc.scalar.activation(th[t][:], b_sb[t][:, :S], ACT.Tanh)
            ga.append(tile(f"ga{t}", [P, S], F32))
            gb.append(tile(f"gb{t}", [P, S], F32))
            prod.append(tile(f"prod{t}", [P, S], F32))

        last = PACK - 1
        for t in range(PACK):
            fetches = [(gb[t], b_sb[t], n4_sb), (ga[t], a_sb[t], n3_sb)]
            for dst, window, places in fetches[::-1] if t == 0 else fetches:
                nc.scalar.activation(dst[:], window[:].indirect(places[:]), ACT.Copy)
            nc.vector.tensor_tensor(prod[t][:], th[t][:], gb[t][:], ALU.mult)
            for js in halves if t == last else [slice(0, S)]:
                nc.vector.tensor_tensor(o_sb[:, t, js], ga[t][:, js], prod[t][:, js], ALU.subtract)
            nc.sync.dma_start(out_rows[:, t, :], o_sb[:, t, :])
            if t == last - 1:
                nc.vector.tensor_copy(ob[:, :, :last], o_sb[:, :last, :].rearrange("p t j -> p j t"))
        for js in halves:
            nc.vector.tensor_copy(ob[:, js, last], o_sb[:, last, js])
        for js in halves:
            nc.vector.quantize_mx(
                out=o_w[:, js].bitcast(FP8X4), scales=o_s[:, js], in_=ob[:, js, :].rearrange("p j t -> p (j t)")
            )
        nc.scalar.dma_start(out_words, o_w[:].bitcast(I32))
        for q in range(QUADS):
            queue = nc.scalar if q < 1 else nc.sync
            queue.dma_start(out_scales[4 * q : 4 * q + 4, :], o_s[32 * q : 32 * q + 4, :].bitcast(I32))
